import numpy as np
import ml_dtypes


def mxq(x, axis, fmt="e4m3"):
    dtype, down = {"e4m3": (ml_dtypes.float8_e4m3fn, 7), "e5m2": (ml_dtypes.float8_e5m2, 14)}[fmt]
    v = np.moveaxis(np.asarray(x, np.float32).astype(ml_dtypes.bfloat16).astype(np.float64), axis, -1)
    blocks = v.reshape(v.shape[:-1] + (-1, 32))
    amax = np.abs(blocks).max(-1, keepdims=True)
    byte = np.maximum(np.where(amax > 0, np.frexp(amax)[1] - 1 + 127, 0) - down, 1)
    scale = np.exp2(byte - 127.0)
    codes = (blocks / scale).astype(np.float32).astype(dtype).astype(np.float64)
    return np.moveaxis((codes * scale).reshape(v.shape), -1, axis)


WIDE = False


def mx_kscale(k):
    if not WIDE:
        return np.ones(k)
    levels = np.array([10, -10, 5, -5, 0])
    if k % 512:
        return np.exp2(np.random.permutation(np.resize(levels, k // 32))).repeat(32)
    a = np.empty((k // 512, 16))
    for p in range(k // 512):
        a[p, :8] = np.random.permutation(np.resize(levels, 8))
        for g in range(8):
            far = levels[np.abs(levels - a[p, g]) >= 10]
            a[p, g + 8] = far[np.random.randint(len(far))]
    return np.exp2(a.ravel()).repeat(32)


def f64(x):
    return np.asarray(x).astype(np.float64)


def striped(idx):
    return np.tile(idx.reshape(-1, 16).T, (8, 1)).astype(np.uint16)


def unstriped(offs):
    return offs[:16].T.reshape(-1).astype(np.int64)


def striped8(idx):
    return np.concatenate([x.reshape(-1, 16).T for x in idx]).astype(np.uint16)


def runs(offs, k):
    lists = np.stack([offs[16 * r : 16 * r + 16].T.reshape(-1) for r in range(8)]).astype(np.int64)
    return lists[np.arange(k) % 512 // 64]


def pack_weight(w):
    k, n = w.shape
    w = f64(np.asarray(w, np.float32).astype(ml_dtypes.bfloat16)).reshape(k // 32, 32, n)
    amax = np.abs(w).max(1)
    byte = np.clip(np.where(amax > 0, np.frexp(amax)[1] - 1 + 127 - 7, 1), 1, 254)
    scaled = (w * np.exp2(127.0 - byte)[:, None, :]).reshape(k, n).astype(np.float32)
    words = np.ascontiguousarray(scaled.reshape(k // 512, 128, 4, n).transpose(0, 1, 3, 2)).astype(ml_dtypes.float8_e4m3fn).view(np.uint8)
    return words, np.ascontiguousarray(byte.astype(np.uint8).reshape(k // 512, 16, n))


def unpack_weight(words, scales):
    g, p, n, _ = words.shape
    vals = np.ascontiguousarray(words).view(ml_dtypes.float8_e4m3fn).astype(np.float64) * np.repeat(np.exp2(scales.astype(np.float64) - 127.0), 8, axis=1)[..., None]
    return vals.transpose(0, 1, 3, 2).reshape(g * 512, n)


def sigmoid(v):
    return 1.0 / (1.0 + np.exp(-np.maximum(v, -700.0)))


K, T, S, N, H = 512, 2048, 256, 512, 512


def setup_inputs():
    n = np.random.standard_normal
    s = mx_kscale(K)[:, None]
    u = mx_kscale(H)
    packed_xT = pack_weight(n((K, T)) * s)
    return {
        "x_words": packed_xT[0],
        "x_scales": packed_xT[1],
        "w1": (n((K, H)) / np.sqrt(K) / s).astype(np.float32),
        "sl": np.random.uniform(1.0, 2.0, (H, 1)).astype(np.float32),
        "th": (0.5 * n((H, 1))).astype(np.float32),
        "gn": (np.random.uniform(0.5, 1.5, (H, 1)) * u[:, None]).astype(np.float32),
        "w2": (n((H, N)) / np.sqrt(H) / u[:, None]).astype(np.float32),
        "w3": (n((K, N)) / np.sqrt(K) / s).astype(np.float32),
        "offs": striped(np.random.permutation(T)[:S]),
        "n1": striped8(np.stack([np.random.permutation(S) for _ in range(8)])),
        "n2": striped8(np.stack([np.random.permutation(S) for _ in range(8)])),
        "two": striped(np.random.permutation(T)[:S]),
        "n3": striped(np.random.permutation(S)),
        "n4": striped(np.random.permutation(S)),
    }


def reference(x_words, x_scales, w1, sl, th, gn, w2, w3, offs, n1, n2, two, n3, n4):
    xq = unpack_weight(x_words, x_scales)[:, unstriped(offs)]
    y = mxq(f64(w1), 0, "e4m3").T @ xq
    sg = sigmoid(f64(sl) * (y[np.arange(H)[:, None], runs(n1, H)] - f64(th)))
    z = f64(gn) * (np.maximum(y * sg, 0.75 * (y[np.arange(H)[:, None], runs(n2, H)])))
    h = mxq(f64(w2), 0, "e4m3").T @ mxq(z, 0, "e4m3")
    x_two = unpack_weight(x_words, x_scales)[:, unstriped(two)]
    d = mxq(f64(w3), 0, "e4m3").T @ x_two
    return 0.75 * (h * d[:, unstriped(n4)] - (h[:, unstriped(n3)] * d))

from contextlib import ExitStack

import concourse.mybir as mybir

K, T, S, N, H = 512, 2048, 256, 512, 512
FLOPS = 2 * S * (K * H + H * N + K * N)

F32 = mybir.dt.float32
BF16 = mybir.dt.bfloat16
I32 = mybir.dt.int32
U32 = mybir.dt.uint32
U16 = mybir.dt.uint16
U8 = mybir.dt.uint8
FP8X4 = mybir.dt.float8_e4m3fn_x4
MULT = mybir.AluOpType.mult
MAX = mybir.AluOpType.max
SUB = mybir.AluOpType.subtract
COPY = mybir.ActivationFunctionType.Copy
SIGMOID = mybir.ActivationFunctionType.Sigmoid

P = 128
PACK = 4
TILES = 4
Y_WINDOW = 2 * S
WINDOW = S + 16


def tile_picked_latecrossbemo_none_p_kernel(
    tc, x_words, x_scales, w1, sl, th, gn, w2, w3, offs, n1, n2, two, n3, n4, out
):
    nc = tc.nc
    with ExitStack() as ctx:
        keep = ctx.enter_context(tc.tile_pool(name="keep", bufs=1))
        psum = ctx.enter_context(tc.psum_pool(name="psum", bufs=1))

        def load_list(name, src):
            tile = keep.tile([P, S // 16], U16, name=name)
            nc.sync.dma_start(tile[:], src)
            return tile

        def load_weight(name, src):
            raw = keep.tile([P, PACK, src.shape[1]], F32, name=name, tag=name)
            nc.sync.dma_start(raw[:], src.rearrange("(p j) c -> p j c", j=PACK))
            return raw

        def load_column(name, src):
            tile = keep.tile([P, TILES], F32, name=name)
            nc.sync.dma_start(tile[:], src.rearrange("(p t) o -> p (t o)", t=TILES))
            return tile

        xs = keep.tile([P, T], U8, name="xs", align_bytes=64)
        nc.gpsimd.memset(xs[:].bitcast(I32), 0)
        offs_t = load_list("offs_t", offs)
        two_t = load_list("two_t", two)
        n1_t = load_list("n1_t", n1)
        n2_t = load_list("n2_t", n2)
        sl_t = load_column("sl_t", sl)
        w1_raw = [load_weight("w1_raw%d" % half, w1[:, half * (H // 2) : (half + 1) * (H // 2)]) for half in range(2)]
        th_t = load_column("th_t", th)
        for q in range(4):
            nc.sync.dma_start(
                xs[32 * q : 32 * q + 4, :].bitcast(I32), x_scales[0, 4 * q : 4 * q + 4, :].bitcast(I32)
            )
        xw = keep.tile([P, T], I32, name="xw", align_bytes=64)
        nc.sync.dma_start(xw[:], x_words[0].rearrange("p n t -> p (n t)").bitcast(I32))
        w3_raw = load_weight("w3_raw", w3)
        w2_raw = load_weight("w2_raw", w2)
        gn_t = load_column("gn_t", gn)
        n4_t = load_list("n4_t", n4)
        n3_t = load_list("n3_t", n3)

        y_sb = [keep.tile([P, Y_WINDOW], F32, name="y_sb%d" % t) for t in range(TILES)]
        d_sb = [keep.tile([P, WINDOW], F32, name="d_sb%d" % t) for t in range(TILES)]
        h_sb = [keep.tile([P, WINDOW], F32, name="h_sb%d" % t) for t in range(TILES)]
        for tile in y_sb + d_sb + h_sb:
            nc.vector.memset(tile[:, S:], 0.0)

        def gather_bytes(name, lst):
            tile = keep.tile([P, S], U8, name=name, align_bytes=64)
            nc.vector.tensor_copy(tile[:], xs[:].indirect(lst[:]))
            return tile

        def gather_words(name, lst):
            tile = keep.tile([P, S], U32, name=name, align_bytes=64)
            nc.vector.tensor_copy(tile[:], xw[:].bitcast(U32).indirect(lst[:]))
            return tile

        def quantize(name, grouped):
            width = grouped.shape[1] // PACK
            codes = keep.tile([P, width], U32, name=name + "_codes", align_bytes=64)
            scales = keep.tile([P, width], U8, name=name + "_scales", align_bytes=64)
            nc.vector.quantize_mx(out=codes[:].bitcast(FP8X4), scales=scales[:], in_=grouped[:])
            return codes, scales

        def product(acc, weight, col, words, scale_bytes):
            codes, scales = weight
            nc.tensor.matmul_mx(
                out=acc,
                lhsT=codes[:, col : col + P].bitcast(FP8X4),
                lhsT_scale=scales[:, col : col + P],
                rhs=words[:].bitcast(FP8X4),
                rhs_scale=scale_bytes[:],
                start=True,
                stop=True,
            )

        w1_bf = keep.tile([P, H * PACK], BF16, name="w1_bf", align_bytes=64)
        for half in range(2):
            nc.vector.tensor_copy(
                w1_bf[:].rearrange("p (t m j) -> p m j t", t=TILES, j=PACK)[:, half * (P // 2) : (half + 1) * (P // 2)],
                w1_raw[half][:].rearrange("p j (m t) -> p m j t", t=TILES),
            )
        xa_s = gather_bytes("xa_s", offs_t)
        w1_q = quantize("w1", w1_bf)
        xb_s = gather_bytes("xb_s", two_t)

        xa_w = gather_words("xa_w", offs_t)
        bias = keep.tile([P, TILES], F32, name="bias")
        nc.vector.scalar_tensor_tensor(bias[:], sl_t[:], -1.0, th_t[:], MULT, MULT)
        xb_w = gather_words("xb_w", two_t)

        y_ps = [psum.tile([P, S], F32, name="y_ps%d" % t, tag="bank%d" % t) for t in range(TILES)]
        for t in range(TILES):
            product(y_ps[t][:], w1_q, t * P, xa_w, xa_s)

        def cast_weight(name, raw):
            grouped = keep.tile([P, 512 * PACK], BF16, name=name, tag=name, align_bytes=64)
            nc.vector.tensor_copy(
                grouped[:].rearrange("p (c i j) -> p c j i", i=4, j=PACK),
                raw[:].rearrange("p j (c i) -> p c j i", i=4),
            )
            return grouped

        sg = [keep.tile([P, S], F32, name="sg%d" % t) for t in range(TILES)]
        yg = [keep.tile([P, S], F32, name="yg%d" % t) for t in range(TILES)]

        for t in range(TILES):
            nc.vector.tensor_copy(y_sb[t][:, :S], y_ps[t][:])
            nc.scalar.activation(
                sg[t][:], y_sb[t][:].indirect(n1_t[:]), SIGMOID, bias=bias[:, t : t + 1], scale=sl_t[:, t : t + 1]
            )
            nc.scalar.activation(yg[t][:], y_sb[t][:].indirect(n2_t[:]), COPY)

        w3_q = quantize("w3", cast_weight("w3_bf", w3_raw))
        d_ps = [psum.tile([P, S], F32, name="d_ps%d" % t, tag="bank%d" % (TILES + t)) for t in range(TILES)]
        for t in range(TILES):
            product(d_ps[t][:], w3_q, t * P, xb_w, xb_s)

        larger = keep.tile([P, TILES, S], F32, name="larger", tag="w3_bf", align_bytes=64)

        def gate(t, tag):
            gated = keep.tile([P, S], F32, name="gated%d" % t, tag=tag)
            nc.vector.tensor_tensor(gated[:], y_ps[t][:], sg[t][:], MULT)
            nc.vector.scalar_tensor_tensor(larger[:, t, :], yg[t][:], 0.75, gated[:], MULT, MAX)

        gate(0, "w3_raw")
        gate(1, "gated1")
        w2_bf = cast_weight("w2_bf", w2_raw)
        gate(2, "w2_raw")
        gate(3, "gated3")

        dg = [keep.tile([P, S], F32, name="dg%d" % t) for t in range(TILES)]
        for t in range(TILES + 1):
            if t < TILES:
                nc.scalar.activation(d_sb[t][:, :S], d_ps[t][:], COPY, scale=0.75)
            if t > 0:
                nc.scalar.activation(dg[t - 1][:], d_sb[t - 1][:].indirect(n4_t[:]), COPY)

        z_bf = keep.tile([P, S * PACK], BF16, name="z_bf", align_bytes=64)
        nc.vector.tensor_tensor(
            z_bf[:].rearrange("p (j t) -> p j t", t=TILES),
            larger[:].rearrange("p t j -> p j t"),
            gn_t[:].unsqueeze(1).to_broadcast([P, S, TILES]),
            MULT,
        )
        w2_q = quantize("w2", w2_bf)
        z_codes, z_scales = quantize("z", z_bf)

        h_ps = [psum.tile([P, S], F32, name="h_ps%d" % t, tag="bank%d" % t) for t in range(TILES)]
        for t in range(TILES):
            product(h_ps[t][:], w2_q, t * P, z_codes, z_scales)

        hg = [keep.tile([P, S], F32, name="hg%d" % t) for t in range(TILES)]
        left = [keep.tile([P, S], F32, name="left%d" % t) for t in range(TILES)]
        right = [keep.tile([P, S], F32, name="right%d" % t) for t in range(TILES)]
        res = [keep.tile([P, S], F32, name="res%d" % t) for t in range(TILES)]

        for t in range(TILES + 1):
            if t < TILES:
                nc.scalar.copy(h_sb[t][:, :S], h_ps[t][:])
                nc.vector.tensor_tensor(left[t][:], h_ps[t][:], dg[t][:], MULT)
            if t > 0:
                nc.scalar.activation(hg[t - 1][:], h_sb[t - 1][:].indirect(n3_t[:]), COPY)
        for t in range(TILES + 1):
            if t < TILES:
                nc.vector.tensor_tensor(right[t][:], hg[t][:], d_sb[t][:, :S], MULT)
            if t > 0:
                nc.vector.tensor_tensor(res[t - 1][:], left[t - 1][:], right[t - 1][:], SUB)
                nc.sync.dma_start(out[(t - 1) * P : t * P, :], res[t - 1][:])
